import numpy as np, ml_dtypes
CORES = [36,164,52,180,100,228,116,244]
N = 8
BF = ml_dtypes.bfloat16
C, V, VX, STEPS = 256, 1024, 2048, 4
def parts(rng):
    x = rng.integers(0, 32, (N, 8, 16, VX), dtype=np.int32); rb = rng.integers(0, V, (N, 8, 16, V), dtype=np.int32)
    a = rng.integers(0, V, (N, 8, 16, C), dtype=np.int32); h = rng.integers(0, 32, (N, 8, 16, C), dtype=np.int32)
    th = rng.integers(80, 135, (N, 8, 16, 1)) + rng.integers(-12, 13, (N, 8, 1, 1)); w = rng.integers(0, 256, (N, 8, 16, 1))
    return x, rb, a, h, th, w
def pack(x, rb, a, h, th, w):
    return {"cues": x.reshape(N, 128, VX).astype(np.float32).astype(BF), "spare": rb.reshape(N, 128, V).astype(np.int32), "scroll": a.reshape(N, 128, C).astype(np.int32),
            "heard": h.reshape(N, 128, C).astype(np.float32).astype(BF), "th": th.reshape(N, 128, 1).astype(np.int32), "w": w.reshape(N, 128, 1).astype(np.int32)}
def setup_inputs(rng):
    return pack(*parts(rng))
def setup_inputs_corners(rng):
    x, rb, a, h, th, w = parts(rng); lane = np.arange(16).reshape(1, 1, 16, 1); n = np.arange(V); c = np.arange(C)
    u = rng.random((N, 8, 1, VX)); x = np.where(u < 0.1, 0, np.where(u < 0.2, 31, x)); u = rng.random((N, 8, 1, C)); h = np.where(u < 0.1, 0, np.where(u < 0.2, 31, h))
    rb = np.choose(rng.integers(0, 5, rb.shape), [0, V - 1, n, (n + 1) % V, rb]); a = np.choose(rng.integers(0, 5, a.shape), [0, V - 1, c, V - C + c, a])
    kd = np.argsort(rng.random((N, 8)), axis=1).reshape(N, 8, 1, 1); j = rng.integers(0, 16, (N, 8, 1, 1)); mid = rng.integers(80, 135, (N, 8, 16, 1))
    th = np.choose(kd, [496, 496 * (lane == 15), 0, 496 * (lane == j), mid, 496 * (lane % 2), mid, mid]); w = np.where(kd == 6, 255, np.where(kd == 7, 0, w))
    q = rng.permutation(N); th[q[0]] = 496; th[q[1]] = 0
    return pack(x, rb, a, h, th, w)
def setup_inputs_ends(rng):
    def two(hi, *shape): return np.where(rng.random(shape) < 0.5, hi, 0)
    lane = np.arange(16).reshape(1, 1, 16, 1)
    u = rng.random((N, 8, 1, VX)); u[..., 1] = 1.0; u[..., V - 2] = 1.0; x = np.where(u < 0.3, 0, np.where(u < 0.6, 31, two(31, N, 8, 16, VX)))
    u = rng.random((N, 8, 1, C)); h = np.where(u < 0.25, 0, np.where(u < 0.5, 31, two(31, N, 8, 16, C)))
    rb = two(V - 1, N, 8, 16, V); u = rng.random((N, 8, 1, V)); rb = np.where(u < 0.1, 0, np.where(u < 0.2, V - 1, rb)); a = two(V - 1, N, 8, 16, C)
    w = two(255, N, 8, 16, 1); w[:, 0, 0] = 0; w[:, 0, 1] = 255; w[:, 7] = 255
    j = rng.integers(0, 16, (N, 8, 1, 1)); only = rng.random((N, 8, 1, 1)) < 0.3; none = rng.random((N, 8, 1, 1)) < 0.4; none[0] = False; none[:, 0] = False; none[N - 1, 7] = True
    th = np.where(lane == j, 496, two(496, N, 8, 16, 1)); th = np.where(only, 496 * (lane == 15), th); th = np.where(none, 0, th); th[:, 0, 0] = 0; th[:, 0, 15] = 496
    s = (16 * 255 * 31) & (VX - 1); x[:, 7, :, s] = 0; x[:, 7, :, (s + V - 1) & (VX - 1)] = 0; x[:, 7, :, V - 2] = 31
    m = rng.random((N, 1, C)) < 0.2; m[..., [0, 1, C - 2, C - 1]] = True; h[:, 7] = np.where(m, 31, h[:, 7])
    return pack(x, rb, a, h, th, w)
def setup_inputs_far(rng):
    x, rb, a, h, th, w = parts(rng); x = rng.integers(20, 32, x.shape); h = rng.integers(0, 4, h.shape)
    half = np.argsort(rng.random((N, 8)), axis=1).reshape(N, 8, 1, 1) & 1
    th = np.where(half == 1, rng.integers(345, 396, (N, 8, 16, 1)), 0)
    q = int(rng.integers(0, N)); p = (q + 1) % N; b = (q - 1) % N; g0 = int(rng.integers(0, 8)); rest = [g for g in range(8) if g != g0]
    x[b] = rng.integers(0, 4, x[b].shape)
    for r, count in ((q, 3 * C + int(rng.integers(8, 16))), (p, 7 * C)):
        th[r] = rng.integers(40, 65, (8, 16, 1)); hit = np.zeros(7 * C, bool); hit[rng.permutation(7 * C)[:count]] = True; hit = hit.reshape(7, C)
        for i, g in enumerate(rest):
            to = (np.arange(VX) - np.add.reduce(w[r, g] * x[r, g], axis=0)) & (VX - 1); can = np.nonzero(to < V)[0]
            c = np.nonzero(hit[i])[0]; n = can[rng.integers(0, len(can), len(c))]
            h[r, g][:, c] = x[r, g][:, n]; a[r, g, rng.integers(0, 16, len(c)), c] = to[n]
    e = rng.integers(-1, 2, (N, 8, C)); h[:, g0, 0::2] = 30 + e; h[:, g0, 1::2] = 30 - e
    x[:, g0, :, :V] = 31; x[:, g0, :, V:] = 0; w[:, g0] = V // 16
    th[:, g0] = rng.choice(np.array([0, 15, 16, 479, 480]), (N, 16, 1)); th[np.arange(N), g0, rng.integers(0, 15, N)] = 480
    return pack(x, rb, a, h, th, w)
def setup_inputs_spread(rng):
    x, rb, a, h, th, w = parts(rng)
    x = np.minimum((np.exp2(5 * rng.random((N, 8, 1, VX))) * rng.random(x.shape) + 0.5).astype(np.int64), 31); h = np.minimum((np.exp2(5 * rng.random((N, 8, 1, C))) * rng.random(h.shape) + 0.5).astype(np.int64), 31)
    def uneven(top, shape, flip):
        v = np.minimum(np.power(float(top), rng.random(shape)).astype(np.int64), top) - 1
        return np.where(rng.random(flip) < 0.3, top - 1 - v, v)
    rb = uneven(V, rb.shape, (N, 8, 1, V)); a = uneven(V, a.shape, (N, 8, 1, C)); w = uneven(256, w.shape, (N, 8, 1, 1))
    th = np.minimum(uneven(497, th.shape, (N, 8, 16, 1)), rng.choice(np.array([20, 60, 110, 496]), (N, 8, 1, 1)))
    return pack(x, rb, a, h, th, w)
def setup_inputs_ties(rng):
    x, rb, a, h, th, w = parts(rng)
    o = rng.integers(6, 26, (N, 8, 16, 2)); e = rng.integers(-6, 7, (N, 8, 16)); pool = rng.integers(0, 32, (N, 8, 16, 4)); pool[..., 0] = o[..., 0] + e; pool[..., 1] = o[..., 0] - e
    x = np.take_along_axis(pool, rng.integers(0, 4, (N, 8, 1, VX)), 3); h = np.take_along_axis(o, (rng.random((N, 8, 1, C)) < 0.3).astype(np.int64), 3)
    less = np.stack([rng.permutation(8) % 2 for q in range(N)])
    th = np.broadcast_to(np.maximum(np.add.reduce(np.abs(e), axis=2) - less, 0)[:, :, None, None], (N, 8, 16, 1))
    a = np.where(rng.random((N, 8, 1, C)) < 0.25, a[:, :, 3:4], a)
    return pack(x, rb, a, h, th, w)
def check_inputs(d):
    bad = []
    for k, hi in (("cues", 31), ("spare", V - 1), ("scroll", V - 1), ("heard", 31), ("th", 496), ("w", 255)):
        v = np.asarray(d[k]).astype(np.float64)
        if not (np.all(v >= 0) and np.all(v <= hi)): bad.append("range of " + k)
        elif np.any(v != np.floor(v)): bad.append("whole numbers in " + k)
    return bad
def reference(cues, spare, scroll, heard, th, w):
    x = cues.astype(np.float32).astype(np.int32).reshape(N, 8, 16, VX); rb = spare.astype(np.int32).reshape(N, 8, 16, V); gb = np.array(rb)
    a = scroll.astype(np.int32).reshape(N, 8, 16, C); h = heard.astype(np.float32).astype(np.int32).reshape(N, 8, 16, C)
    limit = th.astype(np.int32).reshape(N, 8, 16, 1); weight = w.astype(np.int32).reshape(N, 8, 16, 1)
    head = np.zeros((N, 8, C), np.int32); wait = np.zeros((N, 8, C), np.int32); m = [0] * N; place = np.arange(16, dtype=np.int32)[None, :, None]
    for t in range(STEPS):
        say = []
        for r in range(N):
            old = a[r]; hr = h[r]
            shift = np.add.reduce(weight[r] * hr, axis=1) & (VX - 1)
            at = (old + shift[:, None, :]) & (VX - 1)
            px = np.take_along_axis(x[r], at.reshape(8, 1, 16 * C), 2).reshape(8, 16, 16, C)
            d = np.add.reduce(np.abs(px - hr[:, :, None, :]), axis=1)
            o = (place - head[r][:, None, :]) & 15
            near = d <= limit[r] + (m[r] & 15); got = np.any(near, axis=1)
            k = np.argmin(np.where(near, o, 16 + 16 * d + o), axis=1)
            upto = (k - head[r]) & 15
            ak = np.take_along_axis(old, k[:, None, :], 1)[:, 0]
            xk = np.take_along_axis(px, k[:, None, None, :], 2)[:, :, 0]
            rk = np.take_along_axis(rb[r], ak[:, None, :], 2); gk = np.take_along_axis(gb[r], ak[:, None, :], 2)
            sk = np.take_along_axis(x[r], (ak ^ 1)[:, None, :], 2)
            say.append(np.where(got[:, None, :], sk, np.abs(hr - xk)))
            more = np.where(got, 0, wait[r] + 1); full = more == 2
            new = np.where(got[:, None, :] & (o <= upto[:, None, :]), rk, np.where(full[:, None, :], gk, old))
            gi, ci = np.nonzero(got); gb[r][gi, :, (ak - (ak & (C - 1)))[gi, ci] + ci] = old[gi, :, ci]
            head[r] = np.where(got, (k + 1) & 15, np.where(full, 0, head[r])); wait[r] = np.where(full, 0, more)
            m[r] = int(np.count_nonzero(got)); a[r] = new
        h = np.stack([say[(r - 1 - t % (N - 1)) % N] for r in range(N)])
    return {"ys": a.reshape(N, 128, C).astype(np.float32), "yg": gb.reshape(N, 128, V).astype(np.float32), "yh": h.reshape(N, 128, C).astype(np.float32).astype(BF)}

from concourse.mybir import AluOpType as A, AxisListType, ActivationFunctionType as F

C, V, STEPS = 256, 1024, 4
CH = [128, 128]
SUB = 64
GS = 32
NA = 4
GV = 16
GV0 = 64
FE = "V"
QE = "S"
WIN = 60.0
OV = 10.0
PER = 4000.0
MC = 0
OFFS = {'Vs1': -8200, 'Spx': 1300, 'Sot': -11100, 'Vm1': -7500, 'Vl1': 2200, 'Ppd': -300, 'Ppa': 300, 'Vat': 300, 'Yout': -8100, 'Ppk': -1000, 'Vbias': -7800, 'Vu0': 6400, 'Pph': 300, 'Ssp': 600, 'Ppn': -18900, 'Vls': -1000, 'Vfl': 10200, 'Vgap': -1000, 'Ppy': 600, 'Gh': -7500, 'Vsc': 6000, 'Vkt': 2500, 'Vhw': -9400, 'Ppm': 6000, 'Vz1': 13900, 'Vlo': 200, 'Vz0': 3500, 'Vm0': -2500, 'Vs0': 900, 'Vs4': -23100, 'Vpx': -1300, 'Sq': 4100, 'Vhs': -300, 'Vbom': 8800, 'Vcnt': -1600, 'Vs2': -600, 'Smxa': 300, 'Vgd': 4700, 'Pps': 4100, 'Vhi': 9700, 'Vs5': 700, 'Vdf': -300, 'Vk': 10000, 'Vmd': 2100, 'Vn': 1000, 'Vki': 5000}
TAIL = 0.0
FREE = 0
NCH = len(CH)
C0 = [sum(CH[:j]) for j in range(NCH)]
GAP = 1280
BIG = float(2 ** 25)

SCRATCH = {
    "cx": ("sbuf", [128, 3072], "bfloat16"),
    "ws": ("sbuf", [128, 1280], "bfloat16"),
    "px": ("sbuf", [128, 4096], "bfloat16"),
    "mx": ("sbuf", [128, 4096], "bfloat16"),
    "cw": ("sbuf", [128, GAP + 2304], "float32"),
    "spi": ("sbuf", [128, 1024], "int32"),
    "sci": ("sbuf", [128, 256], "int32"),
    "thi": ("sbuf", [128, 4], "int32"),
    "wi": ("sbuf", [128, 4], "int32"),
    "a0": ("sbuf", [128, 256], "float16"),
    "a1": ("sbuf", [128, 256], "float16"),
    "df": ("sbuf", [128, 256], "float16"),
    "md": ("sbuf", [128, 256], "float16"),
    "gd": ("sbuf", [128, 8, 32], "float16"),
    "fl": ("sbuf", [128, 256], "bfloat16"),
    "qq": ("sbuf", [128, 256], "bfloat16"),
    "ot": ("sbuf", [128, 256], "bfloat16"),
    "ot0": ("sbuf", [128, 128], "bfloat16"),
    "qh0": ("sbuf", [128, 160], "float16"),
    "qh1": ("sbuf", [128, 160], "float16"),
    "qk0": ("sbuf", [128, 160], "float16"),
    "qk1": ("sbuf", [128, 160], "float16"),
    "qb0": ("sbuf", [128, 160], "bfloat16"),
    "qb1": ("sbuf", [128, 160], "bfloat16"),
    "at": ("sbuf", [128, 256], "uint16"),
    "kt": ("sbuf", [128, 256], "float32"),
    "sc": ("sbuf", [128, 256], "float32"),
    "yo": ("sbuf", [128, 256], "float32"),
    "rs": ("sbuf", [128, 128], "float32"),
    "ki": ("sbuf", [128, 16], "int32"),
    "xx": ("sbuf", [128, 3, 16], "int32"),
    "yy": ("sbuf", [128, 3, 16], "float32"),
    "zz": ("sbuf", [128, 5, 16], "int32"),
    "m2": ("sbuf", [128, 2, 16], "float32"),
    "uu": ("sbuf", [128, 5, 16], "uint16"),
    "st": ("sbuf", [128, 8, 16], "float32"),
    "li": ("sbuf", [128, 2, 16], "int32"),
    "ls": ("sbuf", [128, 16], "uint16"),
    "lo": ("sbuf", [128, 16], "uint16"),
    "cc": ("sbuf", [128, 16], "float32"),
    "col": ("sbuf", [128, 16], "float32"),
    "coli": ("sbuf", [128, 8], "int32"),
    "onef": ("sbuf", [128, 160], "float32"),
    "idf": ("sbuf", [128, 160], "float32"),
    "idb": ("sbuf", [128, 128], "bfloat16"),
    "idm": ("sbuf", [128, 128], "bfloat16"),
    "idh": ("sbuf", [128, 128], "float16"),
    "blk": ("sbuf", [128, 128], "float32"),
    "bom": ("sbuf", [128, 128], "bfloat16"),
    "wbl": ("sbuf", [128, 128], "bfloat16"),
    "cf": ("sbuf", [128, 144], "float32"),
    "c1": ("sbuf", [128, 144], "bfloat16"),
    "c2": ("sbuf", [128, 144], "bfloat16"),
    "cm": ("sbuf", [128, 144], "bfloat16"),
    "t1": ("sbuf", [128, 289], "int32"),
    "t2": ("sbuf", [128, 289], "int32"),
    "mt": ("sbuf", [128, 289], "bfloat16"),
    "t3": ("sbuf", [128, 17], "float32"),
    "otb": ("sbuf", [128, 17], "bfloat16"),
}
for _t in range(STEPS + 1):
    SCRATCH["h%d" % _t] = ("sbuf", [128, 256], "bfloat16")
for _t in range(STEPS):
    SCRATCH["sp%d" % _t] = ("sbuf", [128, 256], "bfloat16")
for _j in range(NCH - 1):
    SCRATCH["gx%d" % _j] = ("sbuf", [128, 2304], "float32")
for _b in range(8):
    SCRATCH["p%d" % _b] = ("psum", [128, 16, 32] if _b in (5, 6) else [128, 512], "float32")

SEMAPHORES = (["eV", "eS", "eP", "eG", "sent", "outs", "lh", "lw", "lt", "la", "lc0", "lc1", "lsp", "lg"]
              + ["gc%d" % j for j in range(NCH - 1)]
              + ["ar%d_%d" % (t, j) for t in range(STEPS) for j in range(NCH)])

CY = 1.0
PCY = 0.52
GA = 1.56
LAT = 120.0
REM = 2500.0


def plan(g, T, topo, core, rank):
    ops = []
    ph_ = ["."]
    last_w, readers, bank_cur, bank_prev = {}, {}, {}, {}
    q = {"V": g.vector, "S": g.scalar, "P": g.tensor, "G": g, "Y": g.sync}

    def op(eng, fn, r, w, cost, bank=None, sem=None, val=0, lat=0.0):
        i = len(ops)
        hard, soft = set(), set()
        for k in r:
            if k in last_w:
                hard.add(last_w[k])
        for k in w:
            for j in readers.get(k, []) + ([last_w[k]] if k in last_w else []):
                (soft if ops[j]["e"] == eng and ops[j]["sem"] is None and sem is None else hard).add(j)
        if bank is not None:
            cur = bank_cur.get(bank, [])
            if cur and ops[cur[0]]["e"] != eng:
                bank_prev[bank] = cur
                cur = []
            hard.update(bank_prev.get(bank, []))
            if eng == "P" and cur:
                soft.add(cur[-1])
            bank_cur[bank] = cur + [i]
        if eng == "P":
            soft.update(j for j in hard if ops[j]["e"] == "P")
            hard = set(j for j in hard if ops[j]["e"] != "P")
        for k in r:
            readers.setdefault(k, []).append(i)
        for k in w:
            last_w[k] = i
            readers[k] = []
        ops.append({"e": eng, "fn": fn, "hard": hard, "soft": soft - hard, "cost": cost, "sem": sem, "val": val, "lat": lat,
                    "c": eng + ((w[0][0] if isinstance(w[0], tuple) else w[0]) if w else "out"),
                    "k": eng + ((w[0][0] if isinstance(w[0], tuple) else w[0]) if w else "out") + ph_[0],
                    "w": "".join(str(e) for e in w[0]) if w else "out"})

    def vc(n, f=1.0):
        return OV + max(64, n * f) * CY

    def tt(out, a, b, o, r, w, n, f=2.0, bank=None):
        op("V", lambda: g.vector.tensor_tensor(out, a, b, o), r, w, vc(n, f), bank)

    def ts(out, a, s1, s2, o0, o1, r, w, n, f=1.0, bank=None):
        if s2 is None:
            op("V", lambda: g.vector.tensor_scalar(out, a, s1, None, o0), r, w, vc(n, f), bank)
        else:
            op("V", lambda: g.vector.tensor_scalar(out, a, s1, s2, o0, o1), r, w, vc(n, f), bank)

    def cp(out, a, r, w, n, f=1.0, bank=None):
        op("V", lambda: g.vector.tensor_copy(out, a), r, w, vc(n, f), bank)

    def ms(out, v, w, n, r=()):
        op("V", lambda: g.vector.memset(out, v), list(r), w, vc(n))

    def act(out, a, fu, r, w, n, f=1.0, bank=None, bias=0.0, scale=1.0):
        op("S", lambda: g.scalar.activation(out, a, fu, bias=bias, scale=scale), r, w, 65 + max(64, n * f) * CY, bank)

    def mm(out, l, rh, st, sp, r, w, n, bank, f=1):
        op("P", lambda: g.tensor.matmul(out, l, rh, st, sp), r, w, max(64, n) * f * PCY, bank)

    def dma(eng, pairs, sem, r, w, nbytes):
        def fn():
            for o, i in pairs:
                q[eng].dma_start(o, i).then_inc(T.sem[sem], 16)
        op(eng, fn, r, w, 60.0 * len(pairs), None, sem, 16 * len(pairs), 1800.0 + nbytes / 200.0)

    def iota(out, pat, base, cm, w, n, fl=False):
        if fl:
            op("G", lambda: g.iota(out, pat, base, cm, allow_small_or_imprecise_dtypes=True), [], w, 130 + 2 * n * CY)
        else:
            op("G", lambda: g.iota(out, pat, base, cm), [], w, 130 + 2 * n * CY)

    def sel(out, a, pat, cmp, base, cm, r, w, n):
        op("G", lambda: g.affine_select(out, a, pat, cmp, 0.0, base, cm), r, w, 170 + 2 * n * CY)

    allc = range(NCH)

    def each(name):
        return [(name, j) for j in allc]

    dma("Y", [(T.h0[:], T.heard[:])], "lh", [], [("h", 0, j) for j in allc], 1e5)
    dma("S", [(T.wi[:, 0:1], T.w[:])], "lw", [], ["wi"], 1e4)
    dma("Y", [(T.sci[:], T.scroll[:])], "la", [], ["sci"], 2e5)
    dma("S", [(T.cx[:, 2048:3072], T.cues[:, 1024:2048])], "lc1", [], ["cx2"], 4.5e5)
    dma("Y", [(T.cx[:, 1024:2048], T.cues[:, 0:1024])], "lc0", [], ["cx1"], 7e5)
    dma("S", [(T.thi[:, 0:1], T.th[:])], "lt", [], ["thi"], 7e5)
    dma("Y", [(T.spi[:], T.spare[:])], "lsp", ["cx2"], ["spi"], 6e5)

    col = T.col
    lim = -512.0 if FE == "S" else 1.0
    ms(T.onef[:], 1.0, ["onef"], 160)
    sel(T.blk[:], T.onef[:, 0:128], [[-16, 8], [0, 16]], A.is_ge, 0, 1, ["onef"], ["blk"], 128)
    sel(T.blk[:], T.blk[:], [[16, 8], [0, 16]], A.is_ge, 15, -1, ["blk"], ["blk"], 128)
    sel(T.idf[:], T.onef[:], [[-1, 160]], A.is_equal, 16, 1, ["onef"], ["idf"], 160)
    cp(col[:, 0:1], T.wi[:, 0:1], ["wi"], ["wf"], 1)
    ts(T.wbl[:], T.blk[:], col[:, 0:1], None, A.mult, None, ["blk", "wf"], ["wbl"], 128)
    cp(T.idh[:], T.idf[:, 16:144], ["idf"], ["idh"], 128)
    act(T.idm[:], T.idf[:, 16:144], F.Identity, ["idf"], ["idm"], 128, scale=-1.0)
    act(T.idb[:], T.idf[:, 16:144], F.Copy, ["idf"], ["idb"], 128)
    cp(T.a0[:], T.sci[:], ["sci"], [("a", 0, j) for j in allc], 256)
    cp(T.cx[:, 0:1024], T.cx[:, 2048:3072], ["cx2"], ["cx0"], 1024, 0.5)
    act(T.bom[:], T.blk[:], F.Identity, ["blk"], ["bom"], 128, scale=-1.0)
    for i in range(16 - NA, 16):
        ms(T.bom[:, i:128:16], 0.0, ["bom"], 8, ["bom"])
    ms(T.cf[:], 0.0, ["cf"], 144)
    cp(T.cf[:, 15:128:16], T.blk[:, 15:128:16], ["blk", "cf"], ["cf"], 8)
    act(T.c2[:], T.cf[:], F.Identity, ["cf"], ["c2"], 144, scale=2.0)
    act(T.cm[:], T.cf[:], F.Identity, ["cf"], ["cm"], 144, scale=-1.0)
    if NA:
        act(T.c1[:], T.cf[:], F.Copy, ["cf"], ["c1"], 144)
    iota(T.coli[:, 0:1], [[0, 1]], 0, 1, ["p"], 1)
    ts(T.coli[:, 1:2], T.coli[:, 0:1], 15, None, A.bitwise_and, None, ["p"], ["ploi"], 1)
    ts(T.coli[:, 2:3], T.coli[:, 0:1], 4, 1, A.arith_shift_right, A.bitwise_and, ["p"], ["b4i"], 1)
    cp(col[:, 1:3], T.coli[:, 1:3], ["ploi", "b4i"], ["plo", "b4"], 2)
    ts(col[:, 3:4], col[:, 1:2], 1024.0, None, A.mult, None, ["plo"], ["plk"], 1)
    ts(col[:, 7:8], col[:, 2:3], -1.0, 1.0, A.mult, A.add, ["b4"], ["nb4"], 1)
    for g0, cl in ((0, col[:, 7:8]), (1, col[:, 2:3])):
        ts(T["qh%d" % g0][:], T.idf[:], cl, None, A.mult, None, ["idf", "b4", "nb4"], [("qh", g0)], 160)
        ts(T["qk%d" % g0][:], T.idf[:], cl, 32768.0, A.mult, A.mult, ["idf", "b4", "nb4"], [("qk", g0)], 160)
        act(T["qb%d" % g0][:], T.idf[:], F.Identity, ["idf", "b4", "nb4"], [("qb", g0)], 160, scale=cl)
    ts(col[:, 4:5], T.thi[:, 0:1], lim, None, A.mult, None, ["thi"], ["thn"], 1)
    ms(T.rs[:], 0.0, ["rs"], 128)
    ms(T.rs[:, 0:128:16], BIG, ["rs"], 8, ["rs"])
    act(T.ot0[:], T.onef[:, 0:128], F.Identity, ["onef", "plk"], ["ot0"], 128, scale=col[:, 3:4])
    iota(T.st[:, 7, :], [[16, 16]], 0, 0, ["ci"], 16, True)
    ts(T.cc[:], T.st[:, 7, :], col[:, 1:2], None, A.add, None, ["ci", "plo"], ["cc"], 16)
    for j in allc:
        u0, u1 = C0[j] // 16, (C0[j] + CH[j]) // 16
        ts(T.yy[:, 0, u0:u1], T.cc[:, u0:u1], float(-C0[j]), 16.0, A.add, A.mult, ["cc"], [("c16", j)], 8)
    ts(T.m2[:, 0, :], T.cc[:], 1024.0, None, A.add, None, ["cc"], ["ck"], 16)
    ms(T.yy[:, 2, :], 0.0, each("hs"), 16)
    ms(T.m2[:, 1, :], 16.0, each("hw"), 16)
    ms(T.ws[:, 1024:1280], 0.0, each("y"), 128)
    cp(T.ws[:, 0:1024:2], T.cx[:, 1025:2048:2], ["cx1"], ["sw0"], 512, 0.5)
    cp(T.ws[:, 1:1024:2], T.cx[:, 1024:2048:2], ["cx1"], ["sw1"], 512, 0.5)
    iota(T.t1[:], [[-1, 17], [0, 17]], 16, 1, ["t1"], 289)
    iota(T.t2[:], [[0, 17], [1, 17]], 0, 0, ["t2"], 289)
    ts(T.t1[:], T.t1[:], 15, None, A.bitwise_and, None, ["t1"], ["t1"], 289)
    tt(T.mt[:], T.t2[:], T.t1[:], A.is_ge, ["t1", "t2"], ["mt"], 289)
    ms(T.mt[:, 16:289:17], 0.0, ["mt"], 17, ["mt"])
    iota(T.t3[:], [[1, 17]], 0, 0, ["t3"], 17, True)
    ts(T.otb[:], T.t3[:], col[:, 1:2], 16384.0, A.is_gt, A.mult, ["t3", "plo"], ["otb"], 17)
    ms(T.cw[:, 1024:GAP], 0.0, ["pad"], 256)
    cp(T.cw[:, 0:1024], T.spi[:], ["spi"], ["spare"], 1024)
    dma("Y", [(T.cw[:, GAP:GAP + 1024], T.cw[:, 0:1024])], "lg", ["spare"], ["gap"], 5.2e5)

    N = len(T.cores)
    NM = 16 - NA
    for t in range(STEPS):
        last = t == STEPS - 1
        h, a, an, sp = T["h%d" % t], T["a%d" % (t % 2)], T["a%d" % ((t + 1) % 2)], T["sp%d" % t]
        dst = T.cores[(rank + 1 + t % (N - 1)) % N]
        rid, pid = topo.addr(dst, core)
        mask = topo.mask(core, dst)
        neng = len(topo.engines(core, dst))
        bias = col[:, 4:5] if t == 0 else col[:, 5:6]
        for j in allc:
            c0, n = C0[j], CH[j]
            c1 = c0 + n
            ph_[0] = ".%d%d" % (t, j)
            u0, u1 = c0 // 16, c1 // 16
            m = u1 - u0
            H, Ar, An = ("h", t, j), ("a", t % 2, j), ("a", (t + 1) % 2, j)
            b0, b1, nb = c0 // 32, c1 // 32, n // 32
            hc, ac = h[:, c0:c1], a[:, c0:c1]
            bh, bd = 1 + (t * NCH + j) % 2, 3 + (t * NCH + j) % 2
            ph, pd = T["p%d" % bh], T["p%d" % bd]
            mm(ph[:, 256:256 + n], T.wbl[:], hc, True, True, ["wbl", H], [("ps", bh)], n, bh)
            if QE == "S":
                act(T.qq[:, c0:c1], ph[:, 256:256 + n], F.Identity, [("ps", bh)], [("q", j)], n, 1.0, bh, 262144.0)
            else:
                ts(T.qq[:, c0:c1], ph[:, 256:256 + n], 262144.0, None, A.add, None, [("ps", bh)], [("q", j)], n, 1.0, bh)
            mm(T.p0[:, 256:256 + n], T.wbl[:], hc, True, False, ["wbl", H], ["pa"], n, 0)
            mm(T.p0[:, 256:256 + n], T.idh[:], ac, False, False, ["idh", Ar], ["pa"], n, 0)
            mm(T.p0[:, 256:256 + n], T.idm[:], T.qq[:, c0:c1], False, True, ["idm", ("q", j)], ["pa"], n, 0)
            ts(T.at[:, c0:c1], T.p0[:, 256:256 + n], 263168.0, None, A.add, None, ["pa"], [("at", j)], n, 1.0, 0)
            mm(ph[:, 0:n], T.idb[:], hc, True, True, ["idb", H], [("ph", bh)], n, bh)
            mm(pd[:, 0:n], T.bom[:], hc, True, False, ["bom", H], [("pd", bd)], n, bd)
            subs = [(s, min(s + SUB, c1)) for s in range(c0, c1, SUB)]
            gv = GV0 if t == 0 and j == 0 else GV
            cuts = sorted(set(list(range(c0, c1, GS)) + [c0 + gv, c1]))
            PXS = {s0: [("px", e) for e in range(s0 // 8, s1 // 8)] for s0, s1 in subs}
            PX = [("px", e) for e in range(c0 // 8, c1 // 8)]
            for s0, s1 in zip(cuts[:-1], cuts[1:]):
                wr = [("px", e) for e in range(s0 // 8, s1 // 8)]
                rd = ["cx0", "cx1", "cx2", ("at", j)]
                src = T.cx[:, 0:3072].indirect(T.at[:, s0:s1])
                if s1 <= c0 + gv:
                    cp(T.px[:, 16 * s0:16 * s1], src, rd, wr, 16 * (s1 - s0), GA)
                else:
                    act(T.px[:, 16 * s0:16 * s1], src, F.Copy, rd, wr, 16 * (s1 - s0), GA)
            for si, (s0, s1) in enumerate(subs):
                k = s1 - s0
                o0 = s0 - c0
                for i in range(NM):
                    mm(pd[:, o0:o0 + k], T.cm[:, 15 - i:143 - i], T.px[:, 16 * s0 + i:16 * s1:16], False, False,
                       ["cm"] + PXS[s0], [("pd", bd)], k, bd)
                for i in range(NM):
                    b = 16 * c0 + i * n + o0
                    tt(T.mx[:, b:b + k], T.px[:, 16 * s0 + i:16 * s1:16], ph[:, o0:o0 + k], A.max,
                       PXS[s0] + [("ph", bh)], [("mx", s0, i)], k, 1.0, bh)
                    mm(pd[:, o0:o0 + k], T.c2[:, 15 - i:143 - i], T.mx[:, b:b + k], False,
                       NA == 0 and si == len(subs) - 1 and i == NM - 1, ["c2", ("mx", s0, i)], [("pd", bd)], k, bd)
                per = 512 // k
                for e0 in range(0, NA, per):
                    ne = min(per, NA - e0)
                    for e in range(ne):
                        mm(T.p7[:, e * k:e * k + k], T.idm[:], h[:, s0:s1], True, False, ["idm", H], ["py"], k, 7)
                        mm(T.p7[:, e * k:e * k + k], T.idb[:], T.px[:, 16 * s0 + NM + e0 + e:16 * s1:16], False, True,
                           ["idb"] + PXS[s0], ["py"], k, 7)
                    b = 16 * c0 + NM * n + NA * o0 + e0 * k
                    act(T.mx[:, b:b + ne * k], T.p7[:, 0:ne * k], F.Abs, ["py"], [("mxa", s0, e0)], ne * k, 1.0, 7)
                    for e in range(ne):
                        i = NM + e0 + e
                        mm(pd[:, o0:o0 + k], T.c1[:, 15 - i:143 - i], T.mx[:, b + e * k:b + e * k + k], False,
                           i == 15 and si == len(subs) - 1, ["c1", ("mxa", s0, e0)], [("pd", bd)], k, bd)
            if FE == "S":
                act(T.fl[:, c0:c1], pd[:, 0:n], F.Relu, [("pd", bd), "thn", "bias"], [("fl", j)], n, 1.0, bd, bias, 512.0)
            else:
                ts(T.fl[:, c0:c1], pd[:, 0:n], bias, 512.0, A.is_gt, A.mult, [("pd", bd), "thn", "bias"], [("fl", j)], n, 1.0, bd)
            tt(T.gd[:, b0:b1, :], pd[:, 0:n], T.fl[:, c0:c1], A.min, [("pd", bd), ("fl", j)], [("gd", j)], n, 1.0, bd)
            bk = bd + 2
            pk, PK = T["p%d" % bk], ("pk", bk)
            mm(pk[:, 0:nb, :], T.idb[:], T.ot0[:, 0:n], True, False, ["idb", "ot0"], [PK], n, bk)
            terms = [("qh", a, Ar)] + ([("qb", T.ot, "ot")] if t else []) + [("qk", T.gd, ("gd", j))]
            for qn, src, key in terms:
                for g0 in range(2):
                    for cb in range(2):
                        s = 16 - 16 * (cb - g0)
                        qm = T["%s%d" % (qn, g0)][:, s:s + 128]
                        if qn == "qk":
                            mm(pk[:, 0:nb, 16 * g0:16 * g0 + 16], qm, src[:, b0:b1, 16 * cb:16 * cb + 16],
                               False, g0 + cb == 2, [(qn, g0), key], [PK], n // 2, bk)
                        else:
                            for b in range(nb):
                                e = c0 + 32 * b + 16 * cb
                                mm(pk[:, b, 16 * g0:16 * g0 + 16], qm, src[:, e:e + 16], False, False, [(qn, g0), key], [PK], 16, bk)
            op("V", lambda c0=c0, c1=c1, nb=nb, pk=pk: g.vector.transpose(T.kt[:, c0:c1], pk[:, 0:nb, :]), [PK], [("kt", j)], vc(n), bk)
            op("V", lambda c0=c0, c1=c1, n=n: g.vector.tensor_tensor_scan(T.sc[:, c0:c1], T.rs[:, 0:n], T.kt[:, c0:c1], 0.0, A.add, A.min),
               ["rs", ("kt", j)], [("sc", j)], vc(n))
            ki = T.ki[:, u0:u1]
            cp(ki, T.sc[:, c0 + 15:c1:16], [("sc", j)], [("ki", j)], m)
            ts(T.yy[:, 1, u0:u1], T.sc[:, c0 + 15:c1:16], 32768.0, float(GAP), A.is_ge, A.mult, [("sc", j)], [("ng", j)], m)
            if j == NCH - 1 and not last:
                op("V", lambda: g.vector.tensor_reduce(col[:, 6:7], T.yy[:, 1, :], AxisListType.X, A.add), each("ng"), ["cnt"], vc(16))
                mm(pk[:, 15, 0:1], T.onef[:, 0:128], col[:, 6:7], True, True, ["onef", "cnt"], ["pm"], 1, bk, 4)
                ts(T.coli[:, 4:5], pk[:, 15, 0:1], -1.0 / GAP, 2048.0, A.mult, A.add, ["pm"], ["m0"], 1, 1.0, bk)
            ts(T.xx[:, 0, u0:u1], ki, 10, 15, A.arith_shift_right, A.bitwise_and, [("ki", j)], [("k", j)], m)
            ts(T.xx[:, 1, u0:u1], ki, 1023, None, A.bitwise_and, None, [("ki", j)], [("n", j)], m)
            ts(T.xx[:, 2, u0:u1], ki, 10, None, A.arith_shift_right, None, [("ki", j)], [("hi", j)], m)
            tt(T.zz[:, 0:3, u0:u1], T.xx[:, :, u0:u1], T.yy[:, :, u0:u1], A.add,
               [("k", j), ("n", j), ("hi", j), ("c16", j), ("ng", j), ("hs", j)], [("z0", j)], 3 * m)
            tt(T.zz[:, 3:5, u0:u1], T.zz[:, 1:3, u0:u1], T.m2[:, :, u0:u1], A.min, [("z0", j), "ck", ("hw", j)], [("z1", j)], 2 * m)
            if MC:
                cp(T.uu[:, :, u0:u1], T.zz[:, :, u0:u1], [("z0", j), ("z1", j)], [("u", j), ("u0", j)], 5 * m)
            else:
                cp(T.uu[:, 0:2, u0:u1], T.zz[:, 0:2, u0:u1], [("z0", j)], [("u0", j)], 2 * m)
                cp(T.uu[:, 3:5, u0:u1], T.zz[:, 3:5, u0:u1], [("z1", j)], [("u", j)], 2 * m)
            U0, U = ("u0", j), ("u", j)
            tt(T.ws[:, 1024 + c0:1024 + c1], T.px[:, 16 * c0:16 * c1].indirect(T.uu[:, 0, u0:u1]), hc, A.subtract,
               PX + [U0, H], [("y", j)], n, GA)
            act(sp[:, c0:c1], T.ws[:, 0:1280].indirect(T.uu[:, 3, u0:u1]), F.Abs, ["sw0", "sw1", U] + each("y"), [("sp", t, j)], n, GA)
            sem = "ar%d_%d" % (t, j)
            op("G", lambda t=t, c0=c0, c1=c1, sp=sp, sem=sem, rid=rid, pid=pid, mask=mask:
               g.remote_dma(T["h%d" % (t + 1)][:, c0:c1], sp[:, c0:c1], T.sem[sem], T.sem.sent, pid, rid, mask),
               [("sp", t, j)], [("h", t + 1, j)], 300.0, None, sem, neng, REM)
            if t == 0:
                cp(T.lo[:, u0:u1], T.xx[:, 1, u0:u1], [("n", j)], [("lo", j)], m)
                tt(T.df[:, c0:c1], T.spi[:, 0:1024].indirect(T.lo[:, u0:u1]), ac, A.subtract, ["spi", ("lo", j), Ar], [("df", j)], n, GA)
            else:
                tt(T.df[:, c0:c1], T.cw[:, 0:GAP + 1024].indirect(T.uu[:, 1, u0:u1]), ac, A.subtract,
                   ["spare", "pad", "gap", U0, Ar], [("df", j)], n, GA)
            tt(T.md[:, c0:c1], T.mt[:, 0:289].indirect(T.uu[:, 4, u0:u1]), T.df[:, c0:c1], A.mult, ["mt", U, ("df", j)], [("md", j)], n, GA)
            pn, PN = pk[:, 8:8 + nb, :], ("pn", bk)
            mm(pn, T.idh[:], ac, True, False, ["idh", Ar], [PN], n, bk)
            mm(pn, T.idh[:], T.md[:, c0:c1], False, True, ["idh", ("md", j)], [PN], n, bk)
            if not last:
                cp(an[:, c0:c1], pn, [PN], [An], n, 1.0, bk)
            else:
                act(T.yo[:, c0:c1], pn, F.Copy, [PN], [("yo", j)], n, 1.0, bk)
                ts(T.li[:, 0, u0:u1], T.zz[:, 1, u0:u1], 3840, None, A.bitwise_and, None, [("z0", j)], [("l0", j)], m)
                tt(T.li[:, 1, u0:u1], T.li[:, 0, u0:u1], T.cc[:, u0:u1], A.add, [("l0", j), "cc"], [("l1", j)], m)
                cp(T.ls[:, u0:u1], T.li[:, 1, u0:u1], [("l1", j)], [("ls", j)], m)
                if j < NCH - 1:
                    win, key, off = T["gx%d" % j], ("gx", j), 0
                else:
                    win, key, off = T.cw, "gap", GAP
                cp(win[:, off:off + 2304].indirect(T.ls[:, u0:u1]), ac, [("ls", j), Ar, key], [key], n, 3.8)
                dma("Y", [(T.yg[:, 256 * b + c0:256 * b + c1], win[:, off + 256 * b + c0:off + 256 * b + c1]) for b in range(4)],
                    "outs", [key], [], 2048 * n)
                dma("Y", [(T.ys[:, c0:c1], T.yo[:, c0:c1])], "outs", [("yo", j)], [], 512 * n)
                dma("Y", [(T.yh[:, c0:c1], T.h4[:, c0:c1])], "outs", [("h", STEPS, j)], [], 256 * n)
        if last:
            break
        ng, kk = T.yy[:, 1, :], T.xx[:, 0, :]
        ts(T.coli[:, 5:6], T.coli[:, 4:5], 15, None, A.bitwise_and, None, ["m0"], ["m1"], 1)
        ts(col[:, 5:6], T.coli[:, 5:6], lim, col[:, 4:5], A.mult, A.add, ["m1", "thn"], ["bias"], 1)
        S = [T.st[:, e, :] for e in range(7)]
        tt(S[0], kk, ng, A.subtract, each("k") + each("ng"), ["s0"], 16)
        if t == 0:
            ts(S[2], S[0], -1.0, None, A.max, None, ["s0"], ["s2"], 16)
            ts(S[4], ng, 1.0, None, A.min, None, each("ng"), ["s4"], 16)
        else:
            tt(S[1], S[2] if t == 1 else S[6], ng, A.min, ["s2", "s6"] + each("ng"), ["s1"], 16)
            tt(S[2], S[0], S[1], A.max, ["s0", "s1"], ["s2"], 16)
            tt(S[4], S[3], ng, A.min, ["s3"] + each("ng"), ["s4"], 16)
        ts(T.lo[:], S[2], 1.0, None, A.add, None, ["s2"], each("lo"), 16)
        ts(T.yy[:, 2, :], S[2], 16.0, 16.0, A.mult, A.add, ["s2"], each("hs"), 16)
        ts(S[5], S[2], 17.0, 33.0, A.mult, A.add, ["s2"], ["s5"], 16)
        tt(T.m2[:, 1, :], S[5], S[4], A.subtract, ["s5", "s4"], each("hw"), 16)
        if t < 2:
            ts(S[3], S[4], -1.0, 1.0, A.mult, A.add, ["s4"], ["s3"], 16)
        if t == 1:
            ts(S[1], S[4], -100.0, 99.0, A.mult, A.add, ["s4"], ["s1"], 16)
            tt(S[6], S[2], S[1], A.min, ["s2", "s1"], ["s6"], 16)
        act(T.ot[:], T.otb[:, 0:17].indirect(T.lo[:]), F.Copy, ["otb"] + each("lo"), ["ot"], 256, GA)
        ts(T.li[:, 0, :], T.zz[:, 1, :], 3840, None, A.bitwise_and, None, each("z0"), each("l0"), 16)
        tt(T.li[:, 1, :], T.li[:, 0, :], T.cc[:], A.add, each("l0") + ["cc"], each("l1"), 16)
        cp(T.ls[:], T.li[:, 1, :], each("l1"), each("ls"), 16)
        cp(T.cw[:, GAP:GAP + 2304].indirect(T.ls[:]), a[:], each("ls") + [("a", t % 2, j) for j in allc] + ["gap"], ["gap"], 256, 3.8)
        if t == STEPS - 2:
            for j in range(NCH - 1):
                c0, c1 = C0[j], C0[j] + CH[j]
                dma("Y", [(T["gx%d" % j][:, 256 * b + c0:256 * b + c1], T.cw[:, GAP + 256 * b + c0:GAP + 256 * b + c1]) for b in range(4)],
                    "gc%d" % j, ["gap"], [("gx", j)], 2048 * CH[j])
    return ops, q, STEPS * NCH * neng


def schedule(ops):
    n = len(ops)
    succ = [[] for _ in range(n)]
    for i, o in enumerate(ops):
        for j in o["hard"] | o["soft"]:
            succ[j].append(i)
    prio = [0.0] * n
    for i in range(n - 1, -1, -1):
        o = ops[i]
        prio[i] = o["cost"] + max([o["lat"]] + [prio[s] + (o["lat"] + LAT if i in ops[s]["hard"] else 0.0) for s in succ[i]])
    sends = [i for i in range(n) if ops[i]["e"] == "G" and ops[i]["sem"] is not None]
    for k in range(len(sends) - 1 - FREE, -1, -1):
        near = {sends[k]: 0.0}
        for i in range(sends[k] - 1, -1, -1):
            o = ops[i]
            d = [near[s] + (o["lat"] + LAT if i in ops[s]["hard"] else 0.0) for s in succ[i] if s in near]
            if d:
                near[i] = o["cost"] + max(d)
        for i, d in near.items():
            prio[i] = max(prio[i], d + PER * (len(sends) - k) + TAIL)
    for i in range(n):
        prio[i] += OFFS.get(ops[i]["c"], 0.0) + OFFS.get(ops[i]["k"], 0.0)
    left = [len(o["hard"] | o["soft"]) for o in ops]
    est = [0.0] * n
    free = {}
    ready = [i for i in range(n) if left[i] == 0]
    order, end = [], 0.0
    while ready:
        st = {i: max(est[i], free.get(ops[i]["e"], 0.0)) for i in ready}
        f = min(ready, key=lambda i: (st[i], -prio[i]))
        b = max((i for i in ready if ops[i]["e"] == ops[f]["e"] and st[i] <= st[f] + WIN), key=lambda i: (prio[i], -i))
        o = ops[b]
        fin = st[b] + o["cost"]
        free[o["e"]] = fin
        end = max(end, fin + o["lat"])
        o["t"] = st[b]
        ready.remove(b)
        order.append(b)
        for s in succ[b]:
            est[s] = max(est[s], fin + o["lat"] + LAT if b in ops[s]["hard"] else fin)
            left[s] -= 1
            if left[s] == 0:
                ready.append(s)
    return order, end


def rank_program(g, core, T, topo):
    rank = T.rank_of(core)
    if rank is None:
        return
    ops, q, sent = plan(g, T, topo, core, rank)
    order, end = schedule(ops)
    needed = set()
    for o in ops:
        needed.update(o["hard"])
    count, mark, seen, top = {}, {}, {}, {}
    for i in order:
        o = ops[i]
        want = {}
        for j in o["hard"]:
            s, v = mark[j]
            want[s] = max(want.get(s, 0), v)
        for s, v in want.items():
            if seen.get((o["e"], s), 0) < v:
                q[o["e"]].wait_ge(T.sem[s], v)
                seen[(o["e"], s)] = v
                top[s] = max(top.get(s, 0), v)
        ins = o["fn"]()
        if o["sem"] is not None:
            s = o["sem"]
            count[s] = count.get(s, 0) + o["val"]
            mark[i] = (s, count[s])
        elif i in needed:
            s = "e" + o["e"]
            ins.then_inc(T.sem[s], 1)
            count[s] = count.get(s, 0) + 1
            mark[i] = (s, count[s])
    count["sent"] = sent
    for s, v in count.items():
        if top.get(s, 0) < v:
            g.wait_ge(T.sem[s], v)
